import numpy as np
import ml_dtypes


def mxq(x, axis, fmt="e4m3"):
    dtype, down = {"e4m3": (ml_dtypes.float8_e4m3fn, 7), "e5m2": (ml_dtypes.float8_e5m2, 14)}[fmt]
    v = np.moveaxis(np.asarray(x, np.float32).astype(ml_dtypes.bfloat16).astype(np.float64), axis, -1)
    blocks = v.reshape(v.shape[:-1] + (-1, 32))
    amax = np.abs(blocks).max(-1, keepdims=True)
    byte = np.maximum(np.where(amax > 0, np.frexp(amax)[1] - 1 + 127, 0) - down, 1)
    scale = np.exp2(byte - 127.0)
    codes = (blocks / scale).astype(np.float32).astype(dtype).astype(np.float64)
    return np.moveaxis((codes * scale).reshape(v.shape), -1, axis)


WIDE = False


def mx_kscale(k):
    if not WIDE:
        return np.ones(k)
    levels = np.array([10, -10, 5, -5, 0])
    if k % 512:
        return np.exp2(np.random.permutation(np.resize(levels, k // 32))).repeat(32)
    a = np.empty((k // 512, 16))
    for p in range(k // 512):
        a[p, :8] = np.random.permutation(np.resize(levels, 8))
        for g in range(8):
            far = levels[np.abs(levels - a[p, g]) >= 10]
            a[p, g + 8] = far[np.random.randint(len(far))]
    return np.exp2(a.ravel()).repeat(32)


def f64(x):
    return np.asarray(x).astype(np.float64)


def striped8(idx):
    return np.concatenate([x.reshape(-1, 16).T for x in idx]).astype(np.uint16)


def runs(offs, k):
    lists = np.stack([offs[16 * r : 16 * r + 16].T.reshape(-1) for r in range(8)]).astype(np.int64)
    return lists[np.arange(k) % 512 // 64]


def pack_weight(w):
    k, n = w.shape
    w = f64(np.asarray(w, np.float32).astype(ml_dtypes.bfloat16)).reshape(k // 32, 32, n)
    amax = np.abs(w).max(1)
    byte = np.clip(np.where(amax > 0, np.frexp(amax)[1] - 1 + 127 - 7, 1), 1, 254)
    scaled = (w * np.exp2(127.0 - byte)[:, None, :]).reshape(k, n).astype(np.float32)
    words = np.ascontiguousarray(scaled.reshape(k // 512, 128, 4, n).transpose(0, 1, 3, 2)).astype(ml_dtypes.float8_e4m3fn).view(np.uint8)
    return words, np.ascontiguousarray(byte.astype(np.uint8).reshape(k // 512, 16, n))


def unpack_weight(words, scales):
    g, p, n, _ = words.shape
    vals = np.ascontiguousarray(words).view(ml_dtypes.float8_e4m3fn).astype(np.float64) * np.repeat(np.exp2(scales.astype(np.float64) - 127.0), 8, axis=1)[..., None]
    return vals.transpose(0, 1, 3, 2).reshape(g * 512, n)


K, T, S, H, C = 512, 2048, 512, 512, 512


def setup_inputs():
    n = np.random.standard_normal
    s = mx_kscale(K)[:, None]
    packed_xT = pack_weight(n((K, T)) * s)
    return {
        "x_words": packed_xT[0],
        "x_scales": packed_xT[1],
        "w1": (n((K, H)) / np.sqrt(K) / s).astype(np.float32),
        "gs": (np.random.uniform(0.5, 1.5, (K, 1)) / s).astype(np.float32),
        "offs": striped8(np.random.randint(0, T, (8, S))),
        "n1": striped8(np.stack([np.random.permutation(S) for _ in range(8)])),
        "n2": striped8(np.stack([np.random.permutation(S) for _ in range(8)])),
        "cand": striped8(np.random.randint(0, T, (8, C))),
        "n3": striped8(np.stack([np.random.permutation(S) for _ in range(8)])),
        "n4": striped8(np.stack([np.random.permutation(S) for _ in range(8)])),
    }


def reference(x_words, x_scales, w1, gs, offs, n1, n2, cand, n3, n4):
    x_cand = unpack_weight(x_words, x_scales)[np.arange(K)[:, None], runs(cand, K)]
    xq = unpack_weight(x_words, x_scales)[np.arange(K)[:, None], runs(offs, K)]
    y = mxq(f64(w1), 0, "e4m3").T @ xq
    st = y - (y[np.arange(H)[:, None], runs(n1, H)])
    z = f64(gs) * (st / (np.abs(st[np.arange(H)[:, None], runs(n2, H)]) + 0.5))
    s = 0.0625 * ((x_cand.T @ mxq(z, 0, "e4m3")))
    pa = s[np.arange(C)[:, None], runs(n3, C)]
    pb = s[np.arange(C)[:, None], runs(n4, C)]
    mu = 0.3125 * (s + pa + pb)
    return (s - mu) / (np.sqrt((pa - mu) ** 2 + (pb - mu) ** 2 + 0.25))

@@ -1,0 +1,285 @@
+from contextlib import ExitStack
+
+import concourse.mybir as mybir
+from concourse.masks import make_identity
+
+K, T, S, H, C = 512, 2048, 512, 512, 512
+FLOPS = 2 * K * H * S + 2 * K * C * S
+
+F32 = mybir.dt.float32
+BF16 = mybir.dt.bfloat16
+I32 = mybir.dt.int32
+U32 = mybir.dt.uint32
+U16 = mybir.dt.uint16
+U8 = mybir.dt.uint8
+FP8X4 = mybir.dt.float8_e4m3fn_x4
+ALU = mybir.AluOpType
+ACT = mybir.ActivationFunctionType
+
+P = 128
+PACK = 4
+HALF = S // 2
+LIST_HALF = HALF // 16
+
+
+def tile_picked_hcandhopnstd_none_p_kernel(
+    tc, x_words, x_scales, w1, gs, offs, n1, n2, cand, n3, n4, out
+):
+    nc = tc.nc
+    with ExitStack() as ctx:
+        keep = ctx.enter_context(tc.tile_pool(name="keep", bufs=1))
+        work = ctx.enter_context(tc.tile_pool(name="work", bufs=2))
+        psum = ctx.enter_context(tc.psum_pool(name="psum", bufs=1))
+
+        def load_list(name, src):
+            tile = keep.tile([P, S // 16], U16, name=name)
+            nc.sync.dma_start(tile[:], src)
+            return tile
+
+        def cols(h):
+            return slice(h * HALF, (h + 1) * HALF)
+
+        def looked_up(window, offsets, h):
+            return window[:].indirect(offsets[:, h * LIST_HALF : (h + 1) * LIST_HALF])
+
+        half_c = keep.tile([P, 1], F32)
+        quarter_c = keep.tile([P, 1], F32)
+        warm = keep.tile([P, 1], F32)
+        nc.vector.memset(half_c[:], 0.5)
+        nc.vector.memset(quarter_c[:], 0.25)
+        nc.scalar.activation(warm[:], half_c[:], ACT.Abs_reciprocal_sqrt, bias=half_c[:])
+        place_plane = keep.tile([P, S], U8, align_bytes=64)
+        cand_plane = keep.tile([P, C], U8, align_bytes=64)
+        nc.vector.memset(place_plane[:].bitcast(I32), 0)
+        nc.vector.memset(cand_plane[:].bitcast(I32), 0)
+
+        identity = keep.tile([P, P], F32)
+        make_identity(nc, identity[:])
+
+        offs_t = load_list("offs_t", offs)
+        scale_table = keep.tile([P, T], U8, align_bytes=64)
+        rows = x_scales[0].bitcast(I32).rearrange("(g b) c -> b g c", b=2)
+        for b in range(2):
+            nc.sync.dma_start(scale_table[b:P:2, :].bitcast(I32), rows[b].unsqueeze(1).to_broadcast([8, 8, T // 4]))
+        cand_t = load_list("cand_t", cand)
+        word_table = keep.tile([P, T], U32, align_bytes=64)
+        nc.sync.dma_start(word_table[:].bitcast(I32), x_words[0].rearrange("p n t -> p (n t)").bitcast(I32))
+        w_rows = w1.rearrange("(p j) c -> p j c", j=PACK)
+        w_raw = []
+        for h in range(2):
+            w_half = keep.tile([P, PACK, H // 2], F32, name="w_half%d" % h)
+            nc.sync.dma_start(w_half[:], w_rows[:, :, h * (H // 2) : (h + 1) * (H // 2)])
+            w_raw.append(w_half)
+        gs_t = keep.tile([P, PACK], F32)
+        nc.gpsimd.dma_start(gs_t[:], gs.rearrange("(p t) o -> p (t o)", t=PACK))
+        n1_t = load_list("n1_t", n1)
+        n2_t = load_list("n2_t", n2)
+        n3_t = load_list("n3_t", n3)
+        n4_t = load_list("n4_t", n4)
+
+        def to_plane(plane, picked):
+            nc.sync.dma_start(plane[0:112, :].bitcast(I32), picked[14:126, :].bitcast(I32))
+
+        place_bytes = keep.tile([P, S], U8, align_bytes=64)
+        nc.vector.tensor_copy(place_bytes[:], scale_table[:].indirect(offs_t[:]))
+        to_plane(place_plane, place_bytes)
+        cand_bytes = keep.tile([P, C], U8, align_bytes=64)
+        nc.vector.tensor_copy(cand_bytes[:], scale_table[:].indirect(cand_t[:]))
+        cand_bytes_dealt = keep.tile([P, C], U8, align_bytes=64)
+        nc.vector.tensor_copy(
+            cand_bytes_dealt[:].bitcast(I32).rearrange("p (t g i) -> p g t i", t=4, g=8),
+            cand_bytes[:].bitcast(I32).rearrange("p (g t i) -> p g t i", t=4, g=8),
+        )
+        to_plane(cand_plane, cand_bytes_dealt)
+        place_words = keep.tile([P, S], U32, align_bytes=64)
+        nc.vector.tensor_copy(place_words[:], word_table[:].indirect(offs_t[:]))
+        cand_words = keep.tile([P, C], U32, align_bytes=64)
+        nc.vector.tensor_copy(cand_words[:], word_table[:].indirect(cand_t[:]))
+        cand_words_dealt = keep.tile([P, C], U32, align_bytes=64)
+        nc.vector.tensor_copy(
+            cand_words_dealt[:].rearrange("p (t g i) -> p g t i", t=4, g=8),
+            cand_words[:].rearrange("p (g t i) -> p g t i", t=4, g=8),
+        )
+
+        gs_safe = keep.tile([P, PACK], F32)
+        gs_inv = keep.tile([P, PACK], F32)
+        nc.vector.scalar_tensor_tensor(gs_safe[:], gs_t[:], 0.0, gs_t[:], ALU.is_equal, ALU.add)
+        nc.vector.reciprocal(gs_inv[:], gs_safe[:])
+
+        w_grouped = keep.tile([P, PACK, P, PACK], BF16, align_bytes=64)
+
+        def group_views(h, m0, m1):
+            dst = w_grouped[:, :, 64 * h + m0 : 64 * h + m1, :].rearrange("p t m j -> p m j t")
+            src = w_raw[h][:, :, 4 * m0 : 4 * m1].rearrange("p j (m t) -> p m j t", t=PACK)
+            return dst, src
+
+        nc.scalar.copy(*group_views(0, 0, 64))
+        nc.scalar.copy(*group_views(1, 0, 24))
+        nc.vector.tensor_copy(*group_views(1, 24, 64))
+        w_codes = keep.tile([P, H], U32, align_bytes=64)
+        w_plane = keep.tile([P, H], U8, align_bytes=64)
+        y_banks = []
+        for t in range(PACK):
+            tc_cols = slice(t * P, (t + 1) * P)
+            nc.vector.quantize_mx(
+                out=w_codes[:, tc_cols].bitcast(FP8X4),
+                scales=w_plane[:, tc_cols],
+                in_=w_grouped[:, t].rearrange("p m j -> p (m j)"),
+            )
+            y_bank = psum.tile([P, S], F32, name="y_bank%d" % t, tag="y_bank%d" % t)
+            nc.tensor.matmul_mx(
+                out=y_bank[:],
+                lhsT=w_codes[:, tc_cols].bitcast(FP8X4),
+                lhsT_scale=w_plane[:, tc_cols],
+                rhs=place_words[:].bitcast(FP8X4),
+                rhs_scale=place_plane[:],
+                start=True,
+                stop=True,
+            )
+            y_banks.append(y_bank)
+
+        z_planes = keep.tile([P, PACK, S], F32)
+        recips, diffs = [], []
+
+        def first_hop(t):
+            y_window = work.tile([P, S], F32, name="y_window")
+            y_plain = work.tile([P, S], F32, name="y_plain")
+            nc.scalar.activation(y_window[:], y_banks[t][:], ACT.Copy, scale=gs_t[:, t : t + 1])
+            if t == 1:
+                nc.scalar.activation(y_plain[:], y_banks[t][:], ACT.Copy, scale=gs_t[:, t : t + 1])
+            else:
+                nc.vector.tensor_copy(y_plain[:], y_window[:])
+            diff = keep.tile([P, S], F32, name="diff%d" % t)
+            for h in range(2):
+                nc.vector.tensor_tensor(diff[:, cols(h)], looked_up(y_window, n1_t, h), y_plain[:, cols(h)], ALU.subtract)
+            diffs.append(diff)
+
+        def denominators(t):
+            size = work.tile([P, S], F32, name="size")
+            root = work.tile([P, S], F32, name="root")
+            recip = keep.tile([P, S], F32, name="recip%d" % t)
+            nc.scalar.activation(size[:], diffs[t][:], ACT.Abs, scale=gs_inv[:, t : t + 1])
+            nc.scalar.activation(root[:], size[:], ACT.Abs_reciprocal_sqrt, bias=half_c[:])
+            nc.scalar.activation(recip[:], root[:], ACT.Square)
+            recips.append(recip)
+
+        def second_hop(t):
+            for h in range(2):
+                nc.vector.tensor_tensor(z_planes[:, t, cols(h)], looked_up(recips[t], n2_t, h), diffs[t][:, cols(h)], ALU.mult)
+
+        first_hop(0)
+        for t in range(1, PACK):
+            first_hop(t)
+            denominators(t - 1)
+            if t > 1:
+                second_hop(t - 2)
+        denominators(PACK - 1)
+        second_hop(PACK - 2)
+        second_hop(PACK - 1)
+
+        s_banks = [psum.tile([P, S], F32, name="s_bank%d" % t) for t in range(PACK)]
+        s_windows = [keep.tile([P, S], F32, name="s_window%d" % t) for t in range(PACK)]
+        for h in range(2):
+            z_grouped = keep.tile([P, HALF, PACK], BF16, name="z_grouped%d" % h, align_bytes=64)
+            dst = z_grouped[:].rearrange("p (c i) t -> p c t i", i=4)
+            src = z_planes[:, :, cols(h)].rearrange("p t (c i) -> p c t i", i=4)
+            if h == 0:
+                nc.scalar.copy(dst, src)
+            else:
+                nc.vector.tensor_copy(dst, src)
+            z_codes = keep.tile([P, HALF], U32, name="z_codes%d" % h, align_bytes=64)
+            z_plane = keep.tile([P, HALF], U8, name="z_plane%d" % h, align_bytes=64)
+            nc.vector.quantize_mx(
+                out=z_codes[:].bitcast(FP8X4), scales=z_plane[:], in_=z_grouped[:].rearrange("p c t -> p (c t)")
+            )
+            for t in range(PACK):
+                tc_cols = slice(t * P, (t + 1) * P)
+                nc.tensor.matmul_mx(
+                    out=s_banks[t][:, cols(h)],
+                    lhsT=cand_words_dealt[:, tc_cols].bitcast(FP8X4),
+                    lhsT_scale=cand_plane[:, tc_cols],
+                    rhs=z_codes[:].bitcast(FP8X4),
+                    rhs_scale=z_plane[:],
+                    start=True,
+                    stop=True,
+                )
+                nc.scalar.copy(s_windows[t][:, cols(h)], s_banks[t][:, cols(h)])
+
+        out_tiles = out.rearrange("(g t i) c -> t g i c", t=4, g=8)
+        state = {}
+
+        def neighbours(t):
+            pa = work.tile([P, S], F32, name="pa")
+            gap = work.tile([P, S], F32, name="gap")
+            for h in range(2):
+                nc.vector.tensor_copy(pa[:, cols(h)], looked_up(s_windows[t], n3_t, h))
+            for h in range(2):
+                nc.vector.tensor_tensor(gap[:, cols(h)], looked_up(s_windows[t], n4_t, h), pa[:, cols(h)], ALU.subtract)
+            gap_sq = work.tile([P, S], F32, name="gap_sq")
+            pair = work.tile([P, S], F32, name="pair")
+            mid = work.tile([P, S], F32, name="mid")
+            top = work.tile([P, S], F32, name="top")
+            mid_sq = work.tile([P, S], F32, name="mid_sq")
+            state[t] = (pa, gap, gap_sq, pair, mid, top, mid_sq)
+
+        def linear(t, c):
+            pa, gap, gap_sq, pair, mid, top, mid_sq = state[t]
+            nc.vector.scalar_tensor_tensor(pair[:, c], pa[:, c], 2.0, gap[:, c], ALU.mult, ALU.add)
+            nc.vector.scalar_tensor_tensor(mid[:, c], s_banks[t][:, c], -5.0 / 3.0, pair[:, c], ALU.mult, ALU.add)
+            nc.vector.scalar_tensor_tensor(top[:, c], s_banks[t][:, c], -2.2, pair[:, c], ALU.mult, ALU.add)
+            nc.scalar.activation(mid_sq[:, c], mid[:, c], ACT.Square, scale=0.375 * 0.0625)
+
+        def spread(t, c):
+            pa, gap, gap_sq, pair, mid, top, mid_sq = state[t]
+            nc.vector.tensor_tensor(pair[:, c], mid_sq[:, c], gap_sq[:, c], ALU.add)
+            nc.scalar.activation(mid[:, c], pair[:, c], ACT.Abs_reciprocal_sqrt, bias=quarter_c[:], scale=0.5)
+
+        def finish(t, c):
+            pa, gap, gap_sq, pair, mid, top, mid_sq = state[t]
+            result = work.tile([P, c.stop - c.start], F32, name="result")
+            nc.vector.scalar_tensor_tensor(result[:], top[:, c], 0.3125 * 0.0625, mid[:, c], ALU.mult, ALU.mult)
+            nc.sync.dma_start(out_tiles[t][:, :, c], result[:])
+
+        def block(b):
+            return slice(b * P, (b + 1) * P)
+
+        def turned_sum(bank, terms):
+            for b in range(S // P):
+                for i, term in enumerate(terms):
+                    nc.tensor.matmul(
+                        bank[:, block(b)], term[:, block(b)], identity[:],
+                        start=(i == 0), stop=(i == len(terms) - 1), is_transpose=True,
+                    )
+
+        def by_transposes(t):
+            pa, gap, gap_sq, pair, mid, top, mid_sq = state[t]
+            own = work.tile([P, S], F32, name="own")
+            nc.scalar.activation(own[:], s_banks[t][:], ACT.Copy, scale=-5.0 / 3.0)
+            nc.vector.scalar_tensor_tensor(pair[:], pa[:], 2.0, gap[:], ALU.mult, ALU.add)
+            nc.vector.scalar_tensor_tensor(top[:], s_banks[t][:], -2.2, pair[:], ALU.mult, ALU.add)
+            gap_bank = psum.tile([P, S], F32, name="gap_bank", tag="y_bank0")
+            turned_sum(gap_bank, [gap])
+            nc.scalar.activation(gap_sq[:], gap_bank[:], ACT.Square, scale=0.0625)
+            mid_bank = psum.tile([P, S], F32, name="mid_bank", tag="y_bank1")
+            turned_sum(mid_bank, [own, pair])
+            nc.scalar.activation(mid_sq[:], mid_bank[:], ACT.Square, scale=0.375 * 0.0625)
+            spread_bank = psum.tile([P, S], F32, name="spread_bank", tag="y_bank2")
+            turned_sum(spread_bank, [gap_sq, mid_sq])
+            nc.scalar.activation(mid[:], spread_bank[:], ACT.Abs_reciprocal_sqrt, bias=quarter_c[:], scale=0.5)
+
+        whole = slice(0, S)
+        last = PACK - 1
+        for t in range(last):
+            neighbours(t)
+            by_transposes(t)
+            if t > 0:
+                finish(t - 1, whole)
+        neighbours(last)
+        nc.scalar.activation(state[last][2][:], state[last][1][:], ACT.Square, scale=0.0625)
+        linear(last, cols(0))
+        finish(last - 1, whole)
+        linear(last, cols(1))
+        spread(last, cols(0))
+        spread(last, cols(1))
+        finish(last, cols(0))
+        finish(last, cols(1))

@@ -42,6 +42,8 @@ def tile_picked_hcandhopnstd_none_p_kernel(
         def looked_up(window, offsets, h):
             return window[:].indirect(offsets[:, h * LIST_HALF : (h + 1) * LIST_HALF])
 
+        gs_t = keep.tile([P, PACK], F32)
+        nc.scalar.dma_start(gs_t[:], gs.rearrange("(p t) o -> p (t o)", t=PACK))
         half_c = keep.tile([P, 1], F32)
         quarter_c = keep.tile([P, 1], F32)
         warm = keep.tile([P, 1], F32)
@@ -70,8 +72,6 @@ def tile_picked_hcandhopnstd_none_p_kernel(
             w_half = keep.tile([P, PACK, H // 2], F32, name="w_half%d" % h)
             nc.sync.dma_start(w_half[:], w_rows[:, :, h * (H // 2) : (h + 1) * (H // 2)])
             w_raw.append(w_half)
-        gs_t = keep.tile([P, PACK], F32)
-        nc.gpsimd.dma_start(gs_t[:], gs.rearrange("(p t) o -> p (t o)", t=PACK))
         n1_t = load_list("n1_t", n1)
         n2_t = load_list("n2_t", n2)
         n3_t = load_list("n3_t", n3)
@@ -93,39 +93,24 @@ def tile_picked_hcandhopnstd_none_p_kernel(
         to_plane(cand_plane, cand_bytes_dealt)
         place_words = keep.tile([P, S], U32, align_bytes=64)
         nc.vector.tensor_copy(place_words[:], word_table[:].indirect(offs_t[:]))
-        cand_words = keep.tile([P, C], U32, align_bytes=64)
-        nc.vector.tensor_copy(cand_words[:], word_table[:].indirect(cand_t[:]))
-        cand_words_dealt = keep.tile([P, C], U32, align_bytes=64)
-        nc.vector.tensor_copy(
-            cand_words_dealt[:].rearrange("p (t g i) -> p g t i", t=4, g=8),
-            cand_words[:].rearrange("p (g t i) -> p g t i", t=4, g=8),
-        )
 
-        gs_safe = keep.tile([P, PACK], F32)
-        gs_inv = keep.tile([P, PACK], F32)
-        nc.vector.scalar_tensor_tensor(gs_safe[:], gs_t[:], 0.0, gs_t[:], ALU.is_equal, ALU.add)
-        nc.vector.reciprocal(gs_inv[:], gs_safe[:])
-
-        w_grouped = keep.tile([P, PACK, P, PACK], BF16, align_bytes=64)
-
-        def group_views(h, m0, m1):
-            dst = w_grouped[:, :, 64 * h + m0 : 64 * h + m1, :].rearrange("p t m j -> p m j t")
-            src = w_raw[h][:, :, 4 * m0 : 4 * m1].rearrange("p j (m t) -> p m j t", t=PACK)
-            return dst, src
-
-        nc.scalar.copy(*group_views(0, 0, 64))
-        nc.scalar.copy(*group_views(1, 0, 24))
-        nc.vector.tensor_copy(*group_views(1, 24, 64))
         w_codes = keep.tile([P, H], U32, align_bytes=64)
         w_plane = keep.tile([P, H], U8, align_bytes=64)
+        w_grouped = []
+        for h, cast in enumerate((nc.scalar.copy, nc.vector.tensor_copy)):
+            w_grouped.append(keep.tile([P, PACK, P // 2, PACK], BF16, name="w_grouped%d" % h, align_bytes=64))
+            cast(w_grouped[h][:].rearrange("p t m j -> p m j t"), w_raw[h][:].rearrange("p j (m t) -> p m j t", t=PACK))
+        for t in range(PACK):
+            for h in range(2):
+                dealt = slice(t * P + h * (P // 2), t * P + (h + 1) * (P // 2))
+                nc.vector.quantize_mx(
+                    out=w_codes[:, dealt].bitcast(FP8X4),
+                    scales=w_plane[:, dealt],
+                    in_=w_grouped[h][:, t].rearrange("p m j -> p (m j)"),
+                )
         y_banks = []
         for t in range(PACK):
             tc_cols = slice(t * P, (t + 1) * P)
-            nc.vector.quantize_mx(
-                out=w_codes[:, tc_cols].bitcast(FP8X4),
-                scales=w_plane[:, tc_cols],
-                in_=w_grouped[:, t].rearrange("p m j -> p (m j)"),
-            )
             y_bank = psum.tile([P, S], F32, name="y_bank%d" % t, tag="y_bank%d" % t)
             nc.tensor.matmul_mx(
                 out=y_bank[:],
@@ -138,148 +123,184 @@ def tile_picked_hcandhopnstd_none_p_kernel(
             )
             y_banks.append(y_bank)
 
+        cand_words = keep.tile([P, C], U32, tag="w_grouped1", align_bytes=64)
+        nc.vector.tensor_copy(cand_words[:], word_table[:].indirect(cand_t[:]))
+
+        gs_safe = keep.tile([P, PACK], F32)
+        gs_inv = keep.tile([P, PACK], F32)
+        nc.vector.scalar_tensor_tensor(gs_safe[:], gs_t[:], 0.0, gs_t[:], ALU.is_equal, ALU.add)
+        nc.vector.reciprocal(gs_inv[:], gs_safe[:])
+
         z_planes = keep.tile([P, PACK, S], F32)
-        recips, diffs = [], []
+        y_windows, y_plains, diffs, recips = {}, {}, {}, {}
+
+        def y_out(t):
+            y_windows[t] = keep.tile([P, S], F32, name="y_window%d" % t)
+            y_plains[t] = keep.tile([P, S], F32, name="y_plain%d" % t, align_bytes=64)
+            nc.scalar.activation(y_windows[t][:], y_banks[t][:], ACT.Copy, scale=gs_t[:, t : t + 1])
+
+        def plain_copy(t):
+            nc.vector.tensor_copy(y_plains[t][:], y_windows[t][:])
 
         def first_hop(t):
-            y_window = work.tile([P, S], F32, name="y_window")
-            y_plain = work.tile([P, S], F32, name="y_plain")
-            nc.scalar.activation(y_window[:], y_banks[t][:], ACT.Copy, scale=gs_t[:, t : t + 1])
-            if t == 1:
-                nc.scalar.activation(y_plain[:], y_banks[t][:], ACT.Copy, scale=gs_t[:, t : t + 1])
-            else:
-                nc.vector.tensor_copy(y_plain[:], y_window[:])
-            diff = keep.tile([P, S], F32, name="diff%d" % t)
+            diffs[t] = keep.tile([P, S], F32, name="diff%d" % t)
             for h in range(2):
-                nc.vector.tensor_tensor(diff[:, cols(h)], looked_up(y_window, n1_t, h), y_plain[:, cols(h)], ALU.subtract)
-            diffs.append(diff)
+                nc.vector.tensor_tensor(
+                    diffs[t][:, cols(h)], looked_up(y_windows[t], n1_t, h), y_plains[t][:, cols(h)], ALU.subtract
+                )
 
         def denominators(t):
             size = work.tile([P, S], F32, name="size")
             root = work.tile([P, S], F32, name="root")
-            recip = keep.tile([P, S], F32, name="recip%d" % t)
-            nc.scalar.activation(size[:], diffs[t][:], ACT.Abs, scale=gs_inv[:, t : t + 1])
-            nc.scalar.activation(root[:], size[:], ACT.Abs_reciprocal_sqrt, bias=half_c[:])
-            nc.scalar.activation(recip[:], root[:], ACT.Square)
-            recips.append(recip)
+            recips[t] = keep.tile([P, S], F32, name="recip%d" % t)
+            for h in range(2):
+                nc.scalar.activation(size[:, cols(h)], diffs[t][:, cols(h)], ACT.Abs, scale=gs_inv[:, t : t + 1])
+            for h in range(2):
+                nc.scalar.activation(root[:, cols(h)], size[:, cols(h)], ACT.Abs_reciprocal_sqrt, bias=half_c[:])
+            for h in range(2):
+                nc.scalar.activation(recips[t][:, cols(h)], root[:, cols(h)], ACT.Square)
 
         def second_hop(t):
-            for h in range(2):
-                nc.vector.tensor_tensor(z_planes[:, t, cols(h)], looked_up(recips[t], n2_t, h), diffs[t][:, cols(h)], ALU.mult)
+            pieces = 4 if t == PACK - 1 else 2
+            for i in range(pieces):
+                c = slice(i * S // pieces, (i + 1) * S // pieces)
+                window = recips[t][:].indirect(n2_t[:, c.start // 16 : c.stop // 16])
+                nc.vector.tensor_tensor(z_planes[:, t, c], window, diffs[t][:, c], ALU.mult)
 
+        y_out(0)
+        y_out(1)
+        nc.scalar.activation(y_plains[1][:], y_banks[1][:], ACT.Copy, scale=gs_t[:, 1:2])
+        y_out(2)
+        y_out(3)
+        plain_copy(0)
         first_hop(0)
-        for t in range(1, PACK):
-            first_hop(t)
-            denominators(t - 1)
-            if t > 1:
-                second_hop(t - 2)
-        denominators(PACK - 1)
-        second_hop(PACK - 2)
-        second_hop(PACK - 1)
+        first_hop(1)
+        plain_copy(2)
+        plain_copy(3)
+        cand_words_dealt = keep.tile([P, C], U32, tag="y_plain0", align_bytes=64)
+        nc.vector.tensor_copy(
+            cand_words_dealt[:].rearrange("p (t g i) -> p g t i", t=4, g=8),
+            cand_words[:].rearrange("p (g t i) -> p g t i", t=4, g=8),
+        )
+        first_hop(2)
+        first_hop(3)
+        for t in range(PACK):
+            denominators(t)
+            second_hop(t)
 
-        s_banks = [psum.tile([P, S], F32, name="s_bank%d" % t) for t in range(PACK)]
         s_windows = [keep.tile([P, S], F32, name="s_window%d" % t) for t in range(PACK)]
-        for h in range(2):
-            z_grouped = keep.tile([P, HALF, PACK], BF16, name="z_grouped%d" % h, align_bytes=64)
-            dst = z_grouped[:].rearrange("p (c i) t -> p c t i", i=4)
-            src = z_planes[:, :, cols(h)].rearrange("p t (c i) -> p c t i", i=4)
-            if h == 0:
+        z_grouped = keep.tile([P, S, PACK], BF16, align_bytes=64)
+        z_codes = keep.tile([P, S], U32, align_bytes=64)
+        z_plane = keep.tile([P, S], U8, align_bytes=64)
+
+        def scores(bank, t, c):
+            nc.tensor.matmul_mx(
+                out=bank[:],
+                lhsT=cand_words_dealt[:, t * P : (t + 1) * P].bitcast(FP8X4),
+                lhsT_scale=cand_plane[:, t * P : (t + 1) * P],
+                rhs=z_codes[:, c].bitcast(FP8X4),
+                rhs_scale=z_plane[:, c],
+                start=True,
+                stop=True,
+            )
+            nc.scalar.copy(s_windows[t][:, c], bank[:])
+
+        quarters = [slice(i * P, (i + 1) * P) for i in range(4)]
+        for i, c in enumerate(quarters):
+            dst = z_grouped[:, c, :].rearrange("p (c i) t -> p c t i", i=4)
+            src = z_planes[:, :, c].rearrange("p t (c i) -> p c t i", i=4)
+            if i < 2:
                 nc.scalar.copy(dst, src)
             else:
                 nc.vector.tensor_copy(dst, src)
-            z_codes = keep.tile([P, HALF], U32, name="z_codes%d" % h, align_bytes=64)
-            z_plane = keep.tile([P, HALF], U8, name="z_plane%d" % h, align_bytes=64)
+        for i in (0, 2, 1, 3):
+            c = quarters[i]
             nc.vector.quantize_mx(
-                out=z_codes[:].bitcast(FP8X4), scales=z_plane[:], in_=z_grouped[:].rearrange("p c t -> p (c t)")
+                out=z_codes[:, c].bitcast(FP8X4), scales=z_plane[:, c], in_=z_grouped[:, c, :].rearrange("p c t -> p (c t)")
             )
-            for t in range(PACK):
-                tc_cols = slice(t * P, (t + 1) * P)
-                nc.tensor.matmul_mx(
-                    out=s_banks[t][:, cols(h)],
-                    lhsT=cand_words_dealt[:, tc_cols].bitcast(FP8X4),
-                    lhsT_scale=cand_plane[:, tc_cols],
-                    rhs=z_codes[:].bitcast(FP8X4),
-                    rhs_scale=z_plane[:],
-                    start=True,
-                    stop=True,
-                )
-                nc.scalar.copy(s_windows[t][:, cols(h)], s_banks[t][:, cols(h)])
+            scores(psum.tile([P, P], F32, name="s_quarter", tag="y_bank%d" % i), 0, c)
 
         out_tiles = out.rearrange("(g t i) c -> t g i c", t=4, g=8)
-        state = {}
+        ring3 = ctx.enter_context(tc.tile_pool(name="ring3", bufs=3))
+        pas, pairs, tops = {}, {}, {}
 
         def neighbours(t):
-            pa = work.tile([P, S], F32, name="pa")
-            gap = work.tile([P, S], F32, name="gap")
+            pas[t] = ring3.tile([P, S], F32, name="pa")
+            pairs[t] = keep.tile([P, S], F32, name="pair%d" % t, tag="top1" if t == 3 else "pair%d" % t)
+            tops[t] = keep.tile([P, S], F32, name="top%d" % t)
             for h in range(2):
-                nc.vector.tensor_copy(pa[:, cols(h)], looked_up(s_windows[t], n3_t, h))
+                nc.vector.tensor_copy(pas[t][:, cols(h)], looked_up(s_windows[t], n3_t, h))
             for h in range(2):
-                nc.vector.tensor_tensor(gap[:, cols(h)], looked_up(s_windows[t], n4_t, h), pa[:, cols(h)], ALU.subtract)
-            gap_sq = work.tile([P, S], F32, name="gap_sq")
-            pair = work.tile([P, S], F32, name="pair")
-            mid = work.tile([P, S], F32, name="mid")
-            top = work.tile([P, S], F32, name="top")
-            mid_sq = work.tile([P, S], F32, name="mid_sq")
-            state[t] = (pa, gap, gap_sq, pair, mid, top, mid_sq)
+                nc.vector.tensor_tensor(pairs[t][:, cols(h)], looked_up(s_windows[t], n4_t, h), pas[t][:, cols(h)], ALU.add)
 
-        def linear(t, c):
-            pa, gap, gap_sq, pair, mid, top, mid_sq = state[t]
-            nc.vector.scalar_tensor_tensor(pair[:, c], pa[:, c], 2.0, gap[:, c], ALU.mult, ALU.add)
-            nc.vector.scalar_tensor_tensor(mid[:, c], s_banks[t][:, c], -5.0 / 3.0, pair[:, c], ALU.mult, ALU.add)
-            nc.vector.scalar_tensor_tensor(top[:, c], s_banks[t][:, c], -2.2, pair[:, c], ALU.mult, ALU.add)
-            nc.scalar.activation(mid_sq[:, c], mid[:, c], ACT.Square, scale=0.375 * 0.0625)
+        def numerator(t, c):
+            nc.vector.scalar_tensor_tensor(tops[t][:, c], s_windows[t][:, c], -2.2, pairs[t][:, c], ALU.mult, ALU.add)
 
-        def spread(t, c):
-            pa, gap, gap_sq, pair, mid, top, mid_sq = state[t]
-            nc.vector.tensor_tensor(pair[:, c], mid_sq[:, c], gap_sq[:, c], ALU.add)
-            nc.scalar.activation(mid[:, c], pair[:, c], ACT.Abs_reciprocal_sqrt, bias=quarter_c[:], scale=0.5)
+        def turned_sum(bank_cols, a, b):
+            for i in range(HALF // P):
+                blk = slice(i * P, (i + 1) * P)
+                nc.tensor.matmul(bank_cols[:, blk], a[:, blk], identity[:], start=True, stop=False, is_transpose=True)
+                nc.tensor.matmul(bank_cols[:, blk], b[:, blk], identity[:], start=False, stop=True, is_transpose=True)
+
+        def square_tiles(h):
+            gap_sq = keep.tile([P, HALF], F32, name="gap_sq%d" % h)
+            mid_sq = keep.tile([P, HALF], F32, name="mid_sq%d" % h)
+            return gap_sq, mid_sq
+
+        def squares(gap_sq, mid_sq, gap, mid):
+            nc.scalar.activation(gap_sq[:], gap, ACT.Square, scale=0.0625)
+            nc.scalar.activation(mid_sq[:], mid, ACT.Square, scale=0.375 * 0.0625)
+
+        def inverse_root(t, h, spread):
+            nc.scalar.activation(pas[t][:, cols(h)], spread, ACT.Abs_reciprocal_sqrt, bias=quarter_c[:], scale=0.5)
+
+        def by_transposes(t, halves):
+            own = work.tile([P, S], F32, name="own")
+            minus_pa = keep.tile([P, S], F32, name="minus_pa")
+            c = slice(0, len(halves) * HALF)
+            nc.scalar.activation(own[:, c], s_windows[t][:, c], ACT.Copy, scale=-5.0 / 3.0)
+            for h in halves:
+                nc.scalar.activation(minus_pa[:, cols(h)], pas[t][:, cols(h)], ACT.Copy, scale=-2.0)
+            sq = []
+            for h in halves:
+                turned = psum.tile([P, S], F32, name="turned", tag="y_bank%d" % h)
+                turned_sum(turned[:, cols(0)], minus_pa[:, cols(h)], pairs[t][:, cols(h)])
+                turned_sum(turned[:, cols(1)], own[:, cols(h)], pairs[t][:, cols(h)])
+                sq.append(square_tiles(h))
+                squares(*sq[h], turned[:, cols(0)], turned[:, cols(1)])
+            for h in halves:
+                spread = psum.tile([P, HALF], F32, name="spread", tag="y_bank%d" % (2 + h))
+                turned_sum(spread[:], sq[h][0][:], sq[h][1][:])
+                inverse_root(t, h, spread[:])
 
         def finish(t, c):
-            pa, gap, gap_sq, pair, mid, top, mid_sq = state[t]
-            result = work.tile([P, c.stop - c.start], F32, name="result")
-            nc.vector.scalar_tensor_tensor(result[:], top[:, c], 0.3125 * 0.0625, mid[:, c], ALU.mult, ALU.mult)
+            result = keep.tile([P, c.stop - c.start], F32, name="result%d_%d" % (t, c.start))
+            nc.vector.scalar_tensor_tensor(result[:], tops[t][:, c], 0.3125 * 0.0625, pas[t][:, c], ALU.mult, ALU.mult)
             nc.sync.dma_start(out_tiles[t][:, :, c], result[:])
-
-        def block(b):
-            return slice(b * P, (b + 1) * P)
-
-        def turned_sum(bank, terms):
-            for b in range(S // P):
-                for i, term in enumerate(terms):
-                    nc.tensor.matmul(
-                        bank[:, block(b)], term[:, block(b)], identity[:],
-                        start=(i == 0), stop=(i == len(terms) - 1), is_transpose=True,
-                    )
-
-        def by_transposes(t):
-            pa, gap, gap_sq, pair, mid, top, mid_sq = state[t]
-            own = work.tile([P, S], F32, name="own")
-            nc.scalar.activation(own[:], s_banks[t][:], ACT.Copy, scale=-5.0 / 3.0)
-            nc.vector.scalar_tensor_tensor(pair[:], pa[:], 2.0, gap[:], ALU.mult, ALU.add)
-            nc.vector.scalar_tensor_tensor(top[:], s_banks[t][:], -2.2, pair[:], ALU.mult, ALU.add)
-            gap_bank = psum.tile([P, S], F32, name="gap_bank", tag="y_bank0")
-            turned_sum(gap_bank, [gap])
-            nc.scalar.activation(gap_sq[:], gap_bank[:], ACT.Square, scale=0.0625)
-            mid_bank = psum.tile([P, S], F32, name="mid_bank", tag="y_bank1")
-            turned_sum(mid_bank, [own, pair])
-            nc.scalar.activation(mid_sq[:], mid_bank[:], ACT.Square, scale=0.375 * 0.0625)
-            spread_bank = psum.tile([P, S], F32, name="spread_bank", tag="y_bank2")
-            turned_sum(spread_bank, [gap_sq, mid_sq])
-            nc.scalar.activation(mid[:], spread_bank[:], ACT.Abs_reciprocal_sqrt, bias=quarter_c[:], scale=0.5)
 
         whole = slice(0, S)
         last = PACK - 1
         for t in range(last):
             neighbours(t)
-            by_transposes(t)
-            if t > 0:
-                finish(t - 1, whole)
+            numerator(t, cols(0))
+            numerator(t, cols(1))
+            by_transposes(t, range(2))
+            scores(psum.tile([P, S], F32, name="s_bank%d" % t), t + 1, whole)
+        finish(0, whole)
+        finish(1, whole)
         neighbours(last)
-        nc.scalar.activation(state[last][2][:], state[last][1][:], ACT.Square, scale=0.0625)
-        linear(last, cols(0))
-        finish(last - 1, whole)
-        linear(last, cols(1))
-        spread(last, cols(0))
-        spread(last, cols(1))
-        finish(last, cols(0))
+        by_transposes(last, range(1))
+        c = cols(1)
+        gap = keep.tile([P, HALF], F32)
+        mid = keep.tile([P, HALF], F32)
+        numerator(last, cols(0))
+        nc.vector.scalar_tensor_tensor(gap[:], pas[last][:, c], -2.0, pairs[last][:, c], ALU.mult, ALU.add)
+        nc.vector.scalar_tensor_tensor(mid[:], s_windows[last][:, c], -5.0 / 3.0, pairs[last][:, c], ALU.mult, ALU.add)
+        gap_sq, mid_sq = square_tiles(1)
+        squares(gap_sq, mid_sq, gap[:], mid[:])
+        numerator(last, cols(1))
+        finish(2, whole)
+        nc.vector.tensor_tensor(gap[:], gap_sq[:], mid_sq[:], ALU.add)
+        inverse_root(last, 1, gap[:])
         finish(last, cols(1))
+        finish(last, cols(0))

@@ -60,10 +60,11 @@ def tile_picked_hcandhopnstd_none_p_kernel(
 
         offs_t = load_list("offs_t", offs)
         scale_table = keep.tile([P, T], U8, align_bytes=64)
-        rows = x_scales[0].bitcast(I32).rearrange("(g b) c -> b g c", b=2)
-        for b in range(2):
-            nc.sync.dma_start(scale_table[b:P:2, :].bitcast(I32), rows[b].unsqueeze(1).to_broadcast([8, 8, T // 4]))
+        rows = x_scales[0].bitcast(I32)
+        nc.sync.dma_start(scale_table[:].bitcast(I32), rows.unsqueeze(1).to_broadcast([16, 8, T // 4]))
         cand_t = load_list("cand_t", cand)
+        n1_t = load_list("n1_t", n1)
+        n2_t = load_list("n2_t", n2)
         word_table = keep.tile([P, T], U32, align_bytes=64)
         nc.sync.dma_start(word_table[:].bitcast(I32), x_words[0].rearrange("p n t -> p (n t)").bitcast(I32))
         w_rows = w1.rearrange("(p j) c -> p j c", j=PACK)
@@ -72,13 +73,14 @@ def tile_picked_hcandhopnstd_none_p_kernel(
             w_half = keep.tile([P, PACK, H // 2], F32, name="w_half%d" % h)
             nc.sync.dma_start(w_half[:], w_rows[:, :, h * (H // 2) : (h + 1) * (H // 2)])
             w_raw.append(w_half)
-        n1_t = load_list("n1_t", n1)
-        n2_t = load_list("n2_t", n2)
         n3_t = load_list("n3_t", n3)
         n4_t = load_list("n4_t", n4)
 
         def to_plane(plane, picked):
-            nc.sync.dma_start(plane[0:112, :].bitcast(I32), picked[14:126, :].bitcast(I32))
+            for q in range(4):
+                nc.sync.dma_start(
+                    plane[32 * q : 32 * q + 4, :].bitcast(I32), picked[32 * q : 32 * q + 32 : 8, :].bitcast(I32)
+                )
 
         place_bytes = keep.tile([P, S], U8, align_bytes=64)
         nc.vector.tensor_copy(place_bytes[:], scale_table[:].indirect(offs_t[:]))
@@ -87,8 +89,8 @@ def tile_picked_hcandhopnstd_none_p_kernel(
         nc.vector.tensor_copy(cand_bytes[:], scale_table[:].indirect(cand_t[:]))
         cand_bytes_dealt = keep.tile([P, C], U8, align_bytes=64)
         nc.vector.tensor_copy(
-            cand_bytes_dealt[:].bitcast(I32).rearrange("p (t g i) -> p g t i", t=4, g=8),
-            cand_bytes[:].bitcast(I32).rearrange("p (g t i) -> p g t i", t=4, g=8),
+            cand_bytes_dealt[:].bitcast(I32).rearrange("p (t g i) -> p g t i", t=4, g=16),
+            cand_bytes[:].bitcast(I32).rearrange("p (g t i) -> p g t i", t=4, g=16),
         )
         to_plane(cand_plane, cand_bytes_dealt)
         place_words = keep.tile([P, S], U32, align_bytes=64)
@@ -131,7 +133,7 @@ def tile_picked_hcandhopnstd_none_p_kernel(
         nc.vector.scalar_tensor_tensor(gs_safe[:], gs_t[:], 0.0, gs_t[:], ALU.is_equal, ALU.add)
         nc.vector.reciprocal(gs_inv[:], gs_safe[:])
 
-        z_planes = keep.tile([P, PACK, S], F32)
+        z_planes = [keep.tile([P, PACK, HALF], F32, name="z_planes%d" % h) for h in range(2)]
         y_windows, y_plains, diffs, recips = {}, {}, {}, {}
 
         def y_out(t):
@@ -152,20 +154,21 @@ def tile_picked_hcandhopnstd_none_p_kernel(
         def denominators(t):
             size = work.tile([P, S], F32, name="size")
             root = work.tile([P, S], F32, name="root")
+            roots = [root[:, cols(0)], root[:, cols(1)] if t < PACK - 1 else z_planes[1][:, PACK - 2]]
             recips[t] = keep.tile([P, S], F32, name="recip%d" % t)
             for h in range(2):
                 nc.scalar.activation(size[:, cols(h)], diffs[t][:, cols(h)], ACT.Abs, scale=gs_inv[:, t : t + 1])
             for h in range(2):
-                nc.scalar.activation(root[:, cols(h)], size[:, cols(h)], ACT.Abs_reciprocal_sqrt, bias=half_c[:])
+                nc.scalar.activation(roots[h], size[:, cols(h)], ACT.Abs_reciprocal_sqrt, bias=half_c[:])
             for h in range(2):
-                nc.scalar.activation(recips[t][:, cols(h)], root[:, cols(h)], ACT.Square)
+                nc.scalar.activation(recips[t][:, cols(h)], roots[h], ACT.Square)
 
-        def second_hop(t):
-            pieces = 4 if t == PACK - 1 else 2
-            for i in range(pieces):
-                c = slice(i * S // pieces, (i + 1) * S // pieces)
-                window = recips[t][:].indirect(n2_t[:, c.start // 16 : c.stop // 16])
-                nc.vector.tensor_tensor(z_planes[:, t, c], window, diffs[t][:, c], ALU.mult)
+        quarters = [slice(i * P, (i + 1) * P) for i in range(4)]
+
+        def second_hop(t, c):
+            window = recips[t][:].indirect(n2_t[:, c.start // 16 : c.stop // 16])
+            h, start = divmod(c.start, HALF)
+            nc.vector.tensor_tensor(z_planes[h][:, t, start : start + c.stop - c.start], window, diffs[t][:, c], ALU.mult)
 
         y_out(0)
         y_out(1)
@@ -179,17 +182,23 @@ def tile_picked_hcandhopnstd_none_p_kernel(
         plain_copy(3)
         cand_words_dealt = keep.tile([P, C], U32, tag="y_plain0", align_bytes=64)
         nc.vector.tensor_copy(
-            cand_words_dealt[:].rearrange("p (t g i) -> p g t i", t=4, g=8),
-            cand_words[:].rearrange("p (g t i) -> p g t i", t=4, g=8),
+            cand_words_dealt[:].rearrange("p (t g i) -> p g t i", t=4, g=16),
+            cand_words[:].rearrange("p (g t i) -> p g t i", t=4, g=16),
         )
         first_hop(2)
         first_hop(3)
         for t in range(PACK):
             denominators(t)
-            second_hop(t)
+        for t in range(2):
+            second_hop(t, cols(0))
+            second_hop(t, cols(1))
+        for h in range(2):
+            second_hop(2, cols(h))
+            second_hop(3, quarters[2 * h])
+            second_hop(3, quarters[2 * h + 1])
 
         s_windows = [keep.tile([P, S], F32, name="s_window%d" % t) for t in range(PACK)]
-        z_grouped = keep.tile([P, S, PACK], BF16, align_bytes=64)
+        ring3 = ctx.enter_context(tc.tile_pool(name="ring3", bufs=3))
         z_codes = keep.tile([P, S], U32, align_bytes=64)
         z_plane = keep.tile([P, S], U8, align_bytes=64)
 
@@ -205,36 +214,34 @@ def tile_picked_hcandhopnstd_none_p_kernel(
             )
             nc.scalar.copy(s_windows[t][:, c], bank[:])
 
-        quarters = [slice(i * P, (i + 1) * P) for i in range(4)]
         for i, c in enumerate(quarters):
-            dst = z_grouped[:, c, :].rearrange("p (c i) t -> p c t i", i=4)
-            src = z_planes[:, :, c].rearrange("p t (c i) -> p c t i", i=4)
-            if i < 2:
-                nc.scalar.copy(dst, src)
-            else:
-                nc.vector.tensor_copy(dst, src)
-        for i in (0, 2, 1, 3):
-            c = quarters[i]
+            z_grouped = ring3.tile([P, P, PACK], BF16, name="z_grouped", align_bytes=64)
+            cast = nc.scalar.copy if i < 3 else nc.vector.tensor_copy
+            cast(
+                z_grouped[:].rearrange("p (c i) t -> p c t i", i=4),
+                z_planes[i // 2][:, :, quarters[i % 2]].rearrange("p t (c i) -> p c t i", i=4),
+            )
             nc.vector.quantize_mx(
-                out=z_codes[:, c].bitcast(FP8X4), scales=z_plane[:, c], in_=z_grouped[:, c, :].rearrange("p c t -> p (c t)")
+                out=z_codes[:, c].bitcast(FP8X4), scales=z_plane[:, c], in_=z_grouped[:].rearrange("p c t -> p (c t)")
             )
             scores(psum.tile([P, P], F32, name="s_quarter", tag="y_bank%d" % i), 0, c)
 
-        out_tiles = out.rearrange("(g t i) c -> t g i c", t=4, g=8)
-        ring3 = ctx.enter_context(tc.tile_pool(name="ring3", bufs=3))
+        out_tiles = out.rearrange("(g t i) c -> t g i c", t=4, g=16)
         pas, pairs, tops = {}, {}, {}
 
         def neighbours(t):
             pas[t] = ring3.tile([P, S], F32, name="pa")
-            pairs[t] = keep.tile([P, S], F32, name="pair%d" % t, tag="top1" if t == 3 else "pair%d" % t)
             tops[t] = keep.tile([P, S], F32, name="top%d" % t)
             for h in range(2):
                 nc.vector.tensor_copy(pas[t][:, cols(h)], looked_up(s_windows[t], n3_t, h))
             for h in range(2):
-                nc.vector.tensor_tensor(pairs[t][:, cols(h)], looked_up(s_windows[t], n4_t, h), pas[t][:, cols(h)], ALU.add)
+                name = "pair%d_%d" % (t, h)
+                pairs[t, h] = keep.tile([P, HALF], F32, name=name)
+                nc.vector.tensor_tensor(pairs[t, h][:], looked_up(s_windows[t], n4_t, h), pas[t][:, cols(h)], ALU.add)
 
-        def numerator(t, c):
-            nc.vector.scalar_tensor_tensor(tops[t][:, c], s_windows[t][:, c], -2.2, pairs[t][:, c], ALU.mult, ALU.add)
+        def numerator(t, h):
+            c = cols(h)
+            nc.vector.scalar_tensor_tensor(tops[t][:, c], s_windows[t][:, c], -2.2, pairs[t, h][:], ALU.mult, ALU.add)
 
         def turned_sum(bank_cols, a, b):
             for i in range(HALF // P):
@@ -254,24 +261,30 @@ def tile_picked_hcandhopnstd_none_p_kernel(
         def inverse_root(t, h, spread):
             nc.scalar.activation(pas[t][:, cols(h)], spread, ACT.Abs_reciprocal_sqrt, bias=quarter_c[:], scale=0.5)
 
-        def by_transposes(t, halves):
-            own = work.tile([P, S], F32, name="own")
-            minus_pa = keep.tile([P, S], F32, name="minus_pa")
-            c = slice(0, len(halves) * HALF)
-            nc.scalar.activation(own[:, c], s_windows[t][:, c], ACT.Copy, scale=-5.0 / 3.0)
-            for h in halves:
-                nc.scalar.activation(minus_pa[:, cols(h)], pas[t][:, cols(h)], ACT.Copy, scale=-2.0)
-            sq = []
-            for h in halves:
-                turned = psum.tile([P, S], F32, name="turned", tag="y_bank%d" % h)
-                turned_sum(turned[:, cols(0)], minus_pa[:, cols(h)], pairs[t][:, cols(h)])
-                turned_sum(turned[:, cols(1)], own[:, cols(h)], pairs[t][:, cols(h)])
-                sq.append(square_tiles(h))
-                squares(*sq[h], turned[:, cols(0)], turned[:, cols(1)])
-            for h in halves:
-                spread = psum.tile([P, HALF], F32, name="spread", tag="y_bank%d" % (2 + h))
-                turned_sum(spread[:], sq[h][0][:], sq[h][1][:])
-                inverse_root(t, h, spread[:])
+        owns, minus_pas, sqs = {}, {}, {}
+
+        def own_term(t):
+            owns[t] = keep.tile([P, S], F32, name="own%d" % t)
+            nc.scalar.activation(owns[t][:], s_windows[t][:], ACT.Copy, scale=-5.0 / 3.0)
+
+        def minus_term(t, h):
+            minus_pas[t, h] = keep.tile([P, HALF], F32, name="minus_pa%d" % h)
+            nc.scalar.activation(minus_pas[t, h][:], pas[t][:, cols(h)], ACT.Copy, scale=-2.0)
+
+        def turned_squares(t, h):
+            turned = psum.tile([P, S], F32, name="turned", tag="y_bank%d" % h)
+            turned_sum(turned[:, cols(0)], minus_pas[t, h][:], pairs[t, h][:])
+            turned_sum(turned[:, cols(1)], owns[t][:, cols(h)], pairs[t, h][:])
+            sqs[t, h] = square_tiles(h)
+            squares(*sqs[t, h], turned[:, cols(0)], turned[:, cols(1)])
+
+        def turned_back(t, h):
+            spread = psum.tile([P, HALF], F32, name="spread", tag="y_bank%d" % (2 + h))
+            turned_sum(spread[:], sqs[t, h][0][:], sqs[t, h][1][:])
+            inverse_root(t, h, spread[:])
+
+        def whole_scores(t):
+            scores(psum.tile([P, S], F32, name="s_bank%d" % t), t, slice(0, S))
 
         def finish(t, c):
             result = keep.tile([P, c.stop - c.start], F32, name="result%d_%d" % (t, c.start))
@@ -280,27 +293,45 @@ def tile_picked_hcandhopnstd_none_p_kernel(
 
         whole = slice(0, S)
         last = PACK - 1
+        own_term(0)
+        neighbours(0)
+        minus_term(0, 0)
+        minus_term(0, 1)
+        whole_scores(1)
+        own_term(1)
+        whole_scores(2)
         for t in range(last):
-            neighbours(t)
-            numerator(t, cols(0))
-            numerator(t, cols(1))
-            by_transposes(t, range(2))
-            scores(psum.tile([P, S], F32, name="s_bank%d" % t), t + 1, whole)
+            numerator(t, 0)
+            numerator(t, 1)
+            ahead = t + 1 < last
+            if ahead:
+                neighbours(t + 1)
+            for h in range(2):
+                turned_squares(t, h)
+                if ahead:
+                    minus_term(t + 1, h)
+            turned_back(t, 0)
+            if t == 0:
+                own_term(2)
+                whole_scores(3)
+            turned_back(t, 1)
         finish(0, whole)
         finish(1, whole)
         neighbours(last)
-        by_transposes(last, range(1))
-        c = cols(1)
-        gap = keep.tile([P, HALF], F32)
-        mid = keep.tile([P, HALF], F32)
-        numerator(last, cols(0))
-        nc.vector.scalar_tensor_tensor(gap[:], pas[last][:, c], -2.0, pairs[last][:, c], ALU.mult, ALU.add)
-        nc.vector.scalar_tensor_tensor(mid[:], s_windows[last][:, c], -5.0 / 3.0, pairs[last][:, c], ALU.mult, ALU.add)
-        gap_sq, mid_sq = square_tiles(1)
-        squares(gap_sq, mid_sq, gap[:], mid[:])
-        numerator(last, cols(1))
+        gap = keep.tile([P, S], F32)
+        mid = keep.tile([P, S], F32)
+        sq = []
+        for h in range(2):
+            c = cols(h)
+            nc.vector.scalar_tensor_tensor(gap[:, c], pas[last][:, c], -2.0, pairs[last, h][:], ALU.mult, ALU.add)
+            nc.vector.scalar_tensor_tensor(mid[:, c], s_windows[last][:, c], -5.0 / 3.0, pairs[last, h][:], ALU.mult, ALU.add)
+            sq.append(square_tiles(h))
+            squares(*sq[h], gap[:, c], mid[:, c])
+        numerator(last, 0)
+        numerator(last, 1)
         finish(2, whole)
-        nc.vector.tensor_tensor(gap[:], gap_sq[:], mid_sq[:], ALU.add)
-        inverse_root(last, 1, gap[:])
-        finish(last, cols(1))
-        finish(last, cols(0))
+        for h in range(2):
+            nc.vector.tensor_tensor(gap[:, cols(h)], sq[h][0][:], sq[h][1][:], ALU.add)
+            inverse_root(last, h, gap[:, cols(h)])
+        for h in range(2):
+            finish(last, cols(h))

from contextlib import ExitStack

import concourse.mybir as mybir
from concourse.masks import make_identity

K, T, S, H, C = 512, 2048, 512, 512, 512
FLOPS = 2 * K * H * S + 2 * K * C * S

F32 = mybir.dt.float32
BF16 = mybir.dt.bfloat16
I32 = mybir.dt.int32
U32 = mybir.dt.uint32
U16 = mybir.dt.uint16
U8 = mybir.dt.uint8
FP8X4 = mybir.dt.float8_e4m3fn_x4
ALU = mybir.AluOpType
ACT = mybir.ActivationFunctionType

P = 128
PACK = 4
HALF = S // 2
LIST_HALF = HALF // 16


def tile_picked_hcandhopnstd_none_p_kernel(
    tc, x_words, x_scales, w1, gs, offs, n1, n2, cand, n3, n4, out
):
    nc = tc.nc
    with ExitStack() as ctx:
        keep = ctx.enter_context(tc.tile_pool(name="keep", bufs=1))
        work = ctx.enter_context(tc.tile_pool(name="work", bufs=2))
        psum = ctx.enter_context(tc.psum_pool(name="psum", bufs=1))

        def load_list(name, src):
            tile = keep.tile([P, S // 16], U16, name=name)
            nc.sync.dma_start(tile[:], src)
            return tile

        def cols(h):
            return slice(h * HALF, (h + 1) * HALF)

        def looked_up(window, offsets, h):
            return window[:].indirect(offsets[:, h * LIST_HALF : (h + 1) * LIST_HALF])

        gs_t = keep.tile([P, PACK], F32)
        nc.scalar.dma_start(gs_t[:], gs.rearrange("(p t) o -> p (t o)", t=PACK))
        half_c = keep.tile([P, 1], F32)
        quarter_c = keep.tile([P, 1], F32)
        warm = keep.tile([P, 1], F32)
        nc.vector.memset(half_c[:], 0.5)
        nc.vector.memset(quarter_c[:], 0.25)
        nc.scalar.activation(warm[:], half_c[:], ACT.Abs_reciprocal_sqrt, bias=half_c[:])
        place_plane = keep.tile([P, S], U8, align_bytes=64)
        cand_plane = keep.tile([P, C], U8, align_bytes=64)
        nc.vector.memset(place_plane[:].bitcast(I32), 0)
        nc.vector.memset(cand_plane[:].bitcast(I32), 0)

        identity = keep.tile([P, P], F32)
        make_identity(nc, identity[:])

        offs_t = load_list("offs_t", offs)
        scale_table = keep.tile([P, T], U8, align_bytes=64)
        rows = x_scales[0].bitcast(I32)
        nc.sync.dma_start(scale_table[:].bitcast(I32), rows.unsqueeze(1).to_broadcast([16, 8, T // 4]))
        cand_t = load_list("cand_t", cand)
        n1_t = load_list("n1_t", n1)
        n2_t = load_list("n2_t", n2)
        word_table = keep.tile([P, T], U32, align_bytes=64)
        nc.sync.dma_start(word_table[:].bitcast(I32), x_words[0].rearrange("p n t -> p (n t)").bitcast(I32))
        w_rows = w1.rearrange("(p j) c -> p j c", j=PACK)
        w_raw = []
        for h in range(2):
            w_half = keep.tile([P, PACK, H // 2], F32, name="w_half%d" % h)
            nc.sync.dma_start(w_half[:], w_rows[:, :, h * (H // 2) : (h + 1) * (H // 2)])
            w_raw.append(w_half)
        n3_t = load_list("n3_t", n3)
        n4_t = load_list("n4_t", n4)

        def to_plane(plane, picked):
            for q in range(4):
                nc.sync.dma_start(
                    plane[32 * q : 32 * q + 4, :].bitcast(I32), picked[32 * q : 32 * q + 32 : 8, :].bitcast(I32)
                )

        place_bytes = keep.tile([P, S], U8, align_bytes=64)
        nc.vector.tensor_copy(place_bytes[:], scale_table[:].indirect(offs_t[:]))
        to_plane(place_plane, place_bytes)
        cand_bytes = keep.tile([P, C], U8, align_bytes=64)
        nc.vector.tensor_copy(cand_bytes[:], scale_table[:].indirect(cand_t[:]))
        cand_bytes_dealt = keep.tile([P, C], U8, align_bytes=64)
        nc.vector.tensor_copy(
            cand_bytes_dealt[:].bitcast(I32).rearrange("p (t g i) -> p g t i", t=4, g=16),
            cand_bytes[:].bitcast(I32).rearrange("p (g t i) -> p g t i", t=4, g=16),
        )
        to_plane(cand_plane, cand_bytes_dealt)
        place_words = keep.tile([P, S], U32, align_bytes=64)
        nc.vector.tensor_copy(place_words[:], word_table[:].indirect(offs_t[:]))

        w_codes = keep.tile([P, H], U32, align_bytes=64)
        w_plane = keep.tile([P, H], U8, align_bytes=64)
        w_grouped = []
        for h, cast in enumerate((nc.scalar.copy, nc.vector.tensor_copy)):
            w_grouped.append(keep.tile([P, PACK, P // 2, PACK], BF16, name="w_grouped%d" % h, align_bytes=64))
            cast(w_grouped[h][:].rearrange("p t m j -> p m j t"), w_raw[h][:].rearrange("p j (m t) -> p m j t", t=PACK))
        for t in range(PACK):
            for h in range(2):
                dealt = slice(t * P + h * (P // 2), t * P + (h + 1) * (P // 2))
                nc.vector.quantize_mx(
                    out=w_codes[:, dealt].bitcast(FP8X4),
                    scales=w_plane[:, dealt],
                    in_=w_grouped[h][:, t].rearrange("p m j -> p (m j)"),
                )
        y_banks = []
        for t in range(PACK):
            tc_cols = slice(t * P, (t + 1) * P)
            y_bank = psum.tile([P, S], F32, name="y_bank%d" % t, tag="y_bank%d" % t)
            nc.tensor.matmul_mx(
                out=y_bank[:],
                lhsT=w_codes[:, tc_cols].bitcast(FP8X4),
                lhsT_scale=w_plane[:, tc_cols],
                rhs=place_words[:].bitcast(FP8X4),
                rhs_scale=place_plane[:],
                start=True,
                stop=True,
            )
            y_banks.append(y_bank)

        cand_words = keep.tile([P, C], U32, tag="w_grouped1", align_bytes=64)
        nc.vector.tensor_copy(cand_words[:], word_table[:].indirect(cand_t[:]))

        gs_safe = keep.tile([P, PACK], F32)
        gs_inv = keep.tile([P, PACK], F32)
        nc.vector.scalar_tensor_tensor(gs_safe[:], gs_t[:], 0.0, gs_t[:], ALU.is_equal, ALU.add)
        nc.vector.reciprocal(gs_inv[:], gs_safe[:])

        z_planes = [keep.tile([P, PACK, HALF], F32, name="z_planes%d" % h) for h in range(2)]
        y_windows, y_plains, diffs, recips = {}, {}, {}, {}

        def y_out(t):
            y_windows[t] = keep.tile([P, S], F32, name="y_window%d" % t)
            y_plains[t] = keep.tile([P, S], F32, name="y_plain%d" % t, align_bytes=64)
            nc.scalar.activation(y_windows[t][:], y_banks[t][:], ACT.Copy, scale=gs_t[:, t : t + 1])

        def plain_copy(t):
            nc.vector.tensor_copy(y_plains[t][:], y_windows[t][:])

        def first_hop(t):
            diffs[t] = keep.tile([P, S], F32, name="diff%d" % t)
            for h in range(2):
                nc.vector.tensor_tensor(
                    diffs[t][:, cols(h)], looked_up(y_windows[t], n1_t, h), y_plains[t][:, cols(h)], ALU.subtract
                )

        def denominators(t):
            size = work.tile([P, S], F32, name="size")
            root = work.tile([P, S], F32, name="root")
            roots = [root[:, cols(0)], root[:, cols(1)] if t < PACK - 1 else z_planes[1][:, PACK - 2]]
            recips[t] = keep.tile([P, S], F32, name="recip%d" % t)
            for h in range(2):
                nc.scalar.activation(size[:, cols(h)], diffs[t][:, cols(h)], ACT.Abs, scale=gs_inv[:, t : t + 1])
            for h in range(2):
                nc.scalar.activation(roots[h], size[:, cols(h)], ACT.Abs_reciprocal_sqrt, bias=half_c[:])
            for h in range(2):
                nc.scalar.activation(recips[t][:, cols(h)], roots[h], ACT.Square)

        quarters = [slice(i * P, (i + 1) * P) for i in range(4)]

        def second_hop(t, c):
            window = recips[t][:].indirect(n2_t[:, c.start // 16 : c.stop // 16])
            h, start = divmod(c.start, HALF)
            nc.vector.tensor_tensor(z_planes[h][:, t, start : start + c.stop - c.start], window, diffs[t][:, c], ALU.mult)

        y_out(0)
        y_out(1)
        nc.scalar.activation(y_plains[1][:], y_banks[1][:], ACT.Copy, scale=gs_t[:, 1:2])
        y_out(2)
        y_out(3)
        plain_copy(0)
        first_hop(0)
        first_hop(1)
        plain_copy(2)
        plain_copy(3)
        cand_words_dealt = keep.tile([P, C], U32, tag="y_plain0", align_bytes=64)
        nc.vector.tensor_copy(
            cand_words_dealt[:].rearrange("p (t g i) -> p g t i", t=4, g=16),
            cand_words[:].rearrange("p (g t i) -> p g t i", t=4, g=16),
        )
        first_hop(2)
        first_hop(3)
        for t in range(PACK):
            denominators(t)
        for t in range(2):
            second_hop(t, cols(0))
            second_hop(t, cols(1))
        for h in range(2):
            second_hop(2, cols(h))
            second_hop(3, quarters[2 * h])
            second_hop(3, quarters[2 * h + 1])

        s_windows = [keep.tile([P, S], F32, name="s_window%d" % t) for t in range(PACK)]
        ring3 = ctx.enter_context(tc.tile_pool(name="ring3", bufs=3))
        z_codes = keep.tile([P, S], U32, align_bytes=64)
        z_plane = keep.tile([P, S], U8, align_bytes=64)

        def scores(bank, t, c):
            nc.tensor.matmul_mx(
                out=bank[:],
                lhsT=cand_words_dealt[:, t * P : (t + 1) * P].bitcast(FP8X4),
                lhsT_scale=cand_plane[:, t * P : (t + 1) * P],
                rhs=z_codes[:, c].bitcast(FP8X4),
                rhs_scale=z_plane[:, c],
                start=True,
                stop=True,
            )
            nc.scalar.copy(s_windows[t][:, c], bank[:])

        for i, c in enumerate(quarters):
            z_grouped = ring3.tile([P, P, PACK], BF16, name="z_grouped", align_bytes=64)
            cast = nc.scalar.copy if i < 3 else nc.vector.tensor_copy
            cast(
                z_grouped[:].rearrange("p (c i) t -> p c t i", i=4),
                z_planes[i // 2][:, :, quarters[i % 2]].rearrange("p t (c i) -> p c t i", i=4),
            )
            nc.vector.quantize_mx(
                out=z_codes[:, c].bitcast(FP8X4), scales=z_plane[:, c], in_=z_grouped[:].rearrange("p c t -> p (c t)")
            )
            scores(psum.tile([P, P], F32, name="s_quarter", tag="y_bank%d" % i), 0, c)

        out_tiles = out.rearrange("(g t i) c -> t g i c", t=4, g=16)
        pas, pairs, tops = {}, {}, {}

        def neighbours(t):
            pas[t] = ring3.tile([P, S], F32, name="pa")
            tops[t] = keep.tile([P, S], F32, name="top%d" % t)
            for h in range(2):
                nc.vector.tensor_copy(pas[t][:, cols(h)], looked_up(s_windows[t], n3_t, h))
            for h in range(2):
                name = "pair%d_%d" % (t, h)
                pairs[t, h] = keep.tile([P, HALF], F32, name=name)
                nc.vector.tensor_tensor(pairs[t, h][:], looked_up(s_windows[t], n4_t, h), pas[t][:, cols(h)], ALU.add)

        def numerator(t, h):
            c = cols(h)
            nc.vector.scalar_tensor_tensor(tops[t][:, c], s_windows[t][:, c], -2.2, pairs[t, h][:], ALU.mult, ALU.add)

        def turned_sum(bank_cols, a, b):
            for i in range(HALF // P):
                blk = slice(i * P, (i + 1) * P)
                nc.tensor.matmul(bank_cols[:, blk], a[:, blk], identity[:], start=True, stop=False, is_transpose=True)
                nc.tensor.matmul(bank_cols[:, blk], b[:, blk], identity[:], start=False, stop=True, is_transpose=True)

        def square_tiles(h):
            gap_sq = keep.tile([P, HALF], F32, name="gap_sq%d" % h)
            mid_sq = keep.tile([P, HALF], F32, name="mid_sq%d" % h)
            return gap_sq, mid_sq

        def squares(gap_sq, mid_sq, gap, mid):
            nc.scalar.activation(gap_sq[:], gap, ACT.Square, scale=0.0625)
            nc.scalar.activation(mid_sq[:], mid, ACT.Square, scale=0.375 * 0.0625)

        def inverse_root(t, h, spread):
            nc.scalar.activation(pas[t][:, cols(h)], spread, ACT.Abs_reciprocal_sqrt, bias=quarter_c[:], scale=0.5)

        owns, minus_pas, sqs = {}, {}, {}

        def own_term(t):
            owns[t] = keep.tile([P, S], F32, name="own%d" % t)
            nc.scalar.activation(owns[t][:], s_windows[t][:], ACT.Copy, scale=-5.0 / 3.0)

        def minus_term(t, h):
            minus_pas[t, h] = keep.tile([P, HALF], F32, name="minus_pa%d" % h)
            nc.scalar.activation(minus_pas[t, h][:], pas[t][:, cols(h)], ACT.Copy, scale=-2.0)

        def turned_squares(t, h):
            turned = psum.tile([P, S], F32, name="turned", tag="y_bank%d" % h)
            turned_sum(turned[:, cols(0)], minus_pas[t, h][:], pairs[t, h][:])
            turned_sum(turned[:, cols(1)], owns[t][:, cols(h)], pairs[t, h][:])
            sqs[t, h] = square_tiles(h)
            squares(*sqs[t, h], turned[:, cols(0)], turned[:, cols(1)])

        def turned_back(t, h):
            spread = psum.tile([P, HALF], F32, name="spread", tag="y_bank%d" % (2 + h))
            turned_sum(spread[:], sqs[t, h][0][:], sqs[t, h][1][:])
            inverse_root(t, h, spread[:])

        def whole_scores(t):
            scores(psum.tile([P, S], F32, name="s_bank%d" % t), t, slice(0, S))

        def finish(t, c):
            result = keep.tile([P, c.stop - c.start], F32, name="result%d_%d" % (t, c.start))
            nc.vector.scalar_tensor_tensor(result[:], tops[t][:, c], 0.3125 * 0.0625, pas[t][:, c], ALU.mult, ALU.mult)
            nc.sync.dma_start(out_tiles[t][:, :, c], result[:])

        whole = slice(0, S)
        last = PACK - 1
        own_term(0)
        neighbours(0)
        minus_term(0, 0)
        minus_term(0, 1)
        whole_scores(1)
        own_term(1)
        whole_scores(2)
        for t in range(last):
            numerator(t, 0)
            numerator(t, 1)
            ahead = t + 1 < last
            if ahead:
                neighbours(t + 1)
            for h in range(2):
                turned_squares(t, h)
                if ahead:
                    minus_term(t + 1, h)
            turned_back(t, 0)
            if t == 0:
                own_term(2)
                whole_scores(3)
            turned_back(t, 1)
        finish(0, whole)
        finish(1, whole)
        neighbours(last)
        gap = keep.tile([P, S], F32)
        mid = keep.tile([P, S], F32)
        sq = []
        for h in range(2):
            c = cols(h)
            nc.vector.scalar_tensor_tensor(gap[:, c], pas[last][:, c], -2.0, pairs[last, h][:], ALU.mult, ALU.add)
            nc.vector.scalar_tensor_tensor(mid[:, c], s_windows[last][:, c], -5.0 / 3.0, pairs[last, h][:], ALU.mult, ALU.add)
            sq.append(square_tiles(h))
            squares(*sq[h], gap[:, c], mid[:, c])
        numerator(last, 0)
        numerator(last, 1)
        finish(2, whole)
        for h in range(2):
            nc.vector.tensor_tensor(gap[:, cols(h)], sq[h][0][:], sq[h][1][:], ALU.add)
            inverse_root(last, h, gap[:, cols(h)])
        for h in range(2):
            finish(last, cols(h))
